import numpy as np
CORES = [4,12,20,28,44,60,76,84,92,108,116,124]
N = 12
T = 2048
def entries(a): return a.T.reshape(-1)
def pack(v, P): return np.ascontiguousarray(np.asarray(v, np.int32).reshape(-1, P).T)
def lists(rng, how):
    h = rng.integers(0, N * T, 8)
    if how == "zero": h[:] = 0
    if how == "blocks": h = T * rng.integers(1, N, 8)
    if how == "last": h[:] = N * T - 1
    if how == "mixed": h = T * rng.choice([q for q in range(N) if q & (q - 1)], 8) + rng.integers(1, T, 8)
    if how == "small": h = rng.integers(1, T, 8)
    h[1:] = 0
    return {"hh": np.broadcast_to(pack(np.concatenate([h, np.zeros(24, np.int64)]), 16), (N, 16, 2)).copy()}
def setup_inputs(rng):
    return dict({"x": rng.standard_normal((N, 128, T), dtype=np.float32)}, **lists(rng, "uniform"))
def setup_inputs_blocks(rng):
    d = setup_inputs(rng); d.update(lists(rng, "blocks"))
    for k in ("x",): d[k] = (d[k].astype(np.float32) * 1048576.0).astype(d[k].dtype)
    return d
def setup_inputs_last(rng):
    d = setup_inputs(rng); d.update(lists(rng, "last"))
    for k in ("x",): d[k] = (d[k].astype(np.float32) * (1 / 1024.0)).astype(d[k].dtype)
    return d
def setup_inputs_mixed(rng):
    d = setup_inputs(rng); d.update(lists(rng, "mixed"))
    return d
def setup_inputs_small(rng):
    d = setup_inputs(rng); d.update(lists(rng, "small"))
    return d
def setup_inputs_zero(rng):
    d = setup_inputs(rng); d.update(lists(rng, "zero"))
    return d
def check_inputs(x):
    bad = []
    if x["hh"].min() < 0 or x["hh"].max() >= N * T: bad.append("hh out of range")
    if entries(x["hh"][0])[1:].any(): bad.append("an entry that should be 0 isn't")
    if not all(np.array_equal(a, x["hh"][0]) for a in x["hh"]): bad.append("hh isn't alike on all ranks")
    return bad
def reference(x, hh):
    h = entries(hh[0]); A = np.concatenate(list(x), axis=1)
    Y = np.roll(A, -int(h[0]), axis=1)
    return {"y": np.stack([Y[:, T * r:T * r + T] for r in range(N)])}

@@ -1,0 +1,313 @@
+from concourse.bass import DstId, RemoteDMATransfer
+from concourse.mybir import AluOpType as A, ActivationFunctionType as F
+
+CORES = 128
+W = 2048
+NR = 12
+WIDTH = {"big": (48, 48, 48, 32), "small": (48, 48, 32, 32)}
+CHUNKS = [
+    [(0, "big", 0), (1, "big", 0), (2, "big", 0), (0, "small", 0), (1, "small", 0)],
+    [(3, "big", 0), (3, "big", 1), (2, "small", 0), (3, "small", 0)],
+    [(0, "big", 1), (1, "big", 1), (2, "big", 1)],
+]
+
+SCRATCH = {
+    "xt": ("sbuf", [128, 2048], "float32"),
+    "rel": ("sbuf", [128, 384], "float32"),
+    "win": ("sbuf", [128, 576], "float32"),
+    "sel": ("sbuf", [128, 576], "float32"),
+    "z": ("sbuf", [128, 2048], "float32"),
+    "yt": ("sbuf", [128, 2048], "float32"),
+    "h1": ("sbuf", [128, 2], "int32"),
+    "hb": ("sbuf", [128, 2], "int32"),
+    "pi": ("sbuf", [128, 2], "int32"),
+    "pf": ("sbuf", [128, 1], "float32"),
+    "fi": ("sbuf", [128, 1], "int32"),
+    "qi": ("sbuf", [128, 1], "int32"),
+    "ff": ("sbuf", [128, 1], "float32"),
+    "qf": ("sbuf", [128, 1], "float32"),
+    "rr": ("sbuf", [128, 36], "float32"),
+    "kk": ("sbuf", [128, 36], "float32"),
+    "cc": ("sbuf", [128, 36], "float32"),
+    "col": ("sbuf", [128, 36], "float32"),
+    "t0": ("sbuf", [128, 36], "float32"),
+    "t1": ("sbuf", [128, 36], "float32"),
+    "t2": ("sbuf", [128, 36], "float32"),
+    "t3": ("sbuf", [128, 36], "float32"),
+    "off": ("sbuf", [128, 36], "uint16"),
+    "rk": ("sbuf", [128, 128], "int32"),
+    "rj": ("sbuf", [128, 128], "int32"),
+    "rm": ("sbuf", [128, 128], "int32"),
+    "roff": ("sbuf", [128, 128], "uint16"),
+}
+SEMAPHORES = ["hld", "hbs", "hs", "gi", "vc", "u0", "u1", "arr", "sa", "sb", "sc", "loc", "x0", "x1", "x2", "zs",
+              "r0", "r1", "r2", "r3", "st"]
+
+
+def make_plan(T, topo):
+    rank_cores = list(T.cores)
+    chips = [topo.chip(c) for c in rank_cores]
+    planes = []
+    for ch in chips:
+        for pl in planes:
+            if topo.same_plane(ch, pl[0]):
+                pl.append(ch)
+                break
+        else:
+            planes.append([ch])
+    planes.sort(key=len)
+    plane = {"small": planes[0], "big": planes[1]}
+    plane_of = {ch: n for n in plane for ch in plane[n]}
+    pairs = {}
+    for rc, ch in zip(rank_cores, chips):
+        mine = [c for c in range(CORES) if topo.chip(c) == ch]
+        ports = [c for c in mine if all(topo.may_write(c, d) for d in rank_cores)]
+        rest = [c for c in mine if c not in ports and c != rc] + [rc]
+        out = []
+        for dd in sorted({topo.die(c) for c in mine}, key=lambda d: d == topo.die(rc)):
+            out += list(zip([c for c in ports if topo.die(c) == dd], [c for c in rest if topo.die(c) == dd]))
+        pairs[ch] = out
+    units, col = {}, 0
+    spans = []
+    for chunk in CHUNKS:
+        start = col
+        for u in chunk:
+            k, pl, half = u
+            w = WIDTH[pl][k]
+            units[u] = (col, w, plane[pl][4 * half:4 * half + 4])
+            col += 4 * w
+        spans.append((start, col))
+    middle = []
+    for u in units:
+        c0, w, chs = units[u]
+        for i, ch in enumerate(chs):
+            middle.append((pairs[ch][u[0]][0], c0 + i * w, w))
+    return rank_cores, chips, plane_of, pairs, units, spans, middle
+
+
+def engines(topo, src, dsts):
+    m = -1
+    for d in dsts:
+        m &= topo.mask(src, d)
+    return [1 << e for e in range(m.bit_length()) if m >> e & 1]
+
+
+def deal(bits, n):
+    size = 1
+    while 2 * size * n <= len(bits):
+        size *= 2
+    sizes, left = [size] * n, len(bits) - size * n
+    for i in range(n):
+        if left >= sizes[i]:
+            left -= sizes[i]
+            sizes[i] *= 2
+    masks, at = [], 0
+    for s in sizes:
+        masks.append(sum(bits[at:at + s]))
+        at += s
+    return masks
+
+
+def count(m):
+    return bin(m).count("1")
+
+
+def copy_to(topo, dst, src_ap, dst_ap, mask, sem):
+    rid, pid, _ = topo.addr(dst)
+    return RemoteDMATransfer(dst_ids=[DstId(rid=rid, pnc=pid)], dma_engine_mask=mask, remote_sem=sem, src=src_ap,
+                             dst=dst_ap)
+
+
+def phase2(idx):
+    a = idx % 3
+    return [a, (a + 1) % 3, (a + 2) % 3]
+
+
+def rank_program(g, core, T, topo):
+    rank_cores, chips, plane_of, pairs, units, spans, middle = make_plan(T, topo)
+    ch = topo.chip(core)
+    if ch not in pairs:
+        return
+    rank = T.rank_of(core)
+    src_rank = chips.index(ch)
+    rc = rank_cores[src_rank]
+    S = T.sem
+    mids = [m[0] for m in middle]
+    loc = [0]
+    vstep = [0]
+
+    def relay(u):
+        pair = pairs[ch][u[0]]
+        return pair[1] if plane_of[ch] == u[1] else pair[0]
+
+    def vdo(ins):
+        ins.then_inc(S.vc, 1)
+        vstep[0] += 1
+
+    def vwait():
+        g.vector.wait_ge(S.vc, vstep[0])
+
+    def send_unit(u, src, at):
+        c0, w, chs = units[u]
+        dsts = [pairs[y][u[0]][0] for y in chs]
+        masks = deal(engines(topo, core, dsts), 4)
+        tr = [copy_to(topo, d, src[:, at + i * w:at + (i + 1) * w], T.win[:, src_rank * w:(src_rank + 1) * w], masks[i],
+                      S.arr) for i, d in enumerate(dsts)]
+        g.remote_dma_fused(tr, local_sem=S.loc)
+        loc[0] += sum(count(m) for m in masks)
+
+    def p15(n):
+        g.vector.wait_ge(S.gi, n)
+        vdo(g.vector.tensor_scalar(T.pi[:, 1:2], T.pi[:, 0:1], 15, None, A.bitwise_and))
+        vwait()
+        vdo(g.vector.tensor_copy(T.pf[:, :], T.pi[:, 1:2]))
+        vwait()
+
+    if rank is not None:
+        g.scalar.dma_start(T.h1[0:1, :], T.hh[0:1, :]).then_inc(S.hld, 16)
+        xs = [S.x0, S.x1, S.x2]
+        for n, q in ((0, g.sync), (1, g.scalar), (2, g.sync)):
+            a, b = spans[n]
+            q.dma_start(T.xt[:, a:b], T.x[:, a:b]).then_inc(xs[n], 16)
+        g.iota(T.pi[:, 0:1], [[0, 1]], 0, 1).then_inc(S.gi, 1)
+        g.iota(T.rk[:, :], [[16, 128]], 0, 0).then_inc(S.gi, 1)
+        g.wait_ge(S.hld, 16)
+        g.partition_broadcast(T.hb[:, :], T.h1[0:1, :], 128).then_inc(S.hbs, 1)
+        g.wait_ge(S.hbs, 1)
+        ports = [p for p, _ in pairs[ch]]
+        m = sum(engines(topo, core, ports))
+        ids = []
+        for p in ports:
+            rid, pid, _ = topo.addr(p)
+            ids.append(DstId(rid=rid, pnc=pid))
+        g.remote_dma_fused([RemoteDMATransfer(dst_ids=ids, dma_engine_mask=m, remote_sem=S.hs, srcs=[T.hb[:, :]],
+                                              dsts=[T.hb[:, :] for p in ports])], local_sem=S.loc)
+        loc[0] += count(m)
+        mine = []
+        for n, chunk in enumerate(CHUNKS):
+            g.wait_ge(xs[n], 16)
+            mine += [u for u in chunk if relay(u) == core]
+            out = [u for u in chunk if relay(u) != core]
+            out.sort(key=lambda u: topo.die(relay(u)) != topo.die(core))
+            bits = engines(topo, core, [relay(u) for u in out])
+            masks = deal(bits[1::2] + bits[0::2], len(out))
+            tr = []
+            for u, mk in zip(out, masks):
+                c0, w, _ = units[u]
+                at = u[2] * 4 * w
+                tr.append(copy_to(topo, relay(u), T.xt[:, c0:c0 + 4 * w], T.rel[:, at:at + 4 * w], mk,
+                                  S["u%d" % u[2]]))
+            g.remote_dma_fused(tr, local_sem=S.loc)
+            loc[0] += sum(count(mk) for mk in masks)
+        for u in mine:
+            send_unit(u, T.xt, units[u][0])
+        p15(2)
+        g.vector.wait_ge(S.hbs, 1)
+        vdo(g.vector.tensor_copy(T.ff[:, :], T.hb[:, 0:1]))
+        vwait()
+        vdo(g.vector.tensor_scalar(T.rj[:, :], T.rk[:, :], T.pf[:, :], T.ff[:, :], A.add, A.add))
+        vwait()
+        vdo(g.vector.tensor_scalar(T.rm[:, :], T.rj[:, :], W - 1, None, A.bitwise_and))
+        vwait()
+        vdo(g.vector.tensor_copy(T.roff[:, :], T.rm[:, :]))
+        vwait()
+        total = 0
+        for idx in range(len(middle)):
+            total += 2 if rank // 4 == phase2(idx)[2] else 1
+        g.vector.wait_ge(S.zs, total)
+        g.scalar.wait_ge(S.vc, vstep[0])
+        g.scalar.wait_ge(S.zs, total)
+        B = W // 4
+        for b in range(4):
+            src = T.z[:, :].indirect(T.roff[:, b * B // 16:(b + 1) * B // 16])
+            dst = T.yt[:, b * B:(b + 1) * B]
+            if b % 2 == 0:
+                g.vector.tensor_copy(dst, src).then_inc(S["r%d" % b], 1)
+            else:
+                g.scalar.activation(dst, src, F.Copy).then_inc(S["r%d" % b], 1)
+        for b in range(4):
+            g.sync.wait_ge(S["r%d" % b], 1)
+            g.sync.dma_start(T.y[:, b * B:(b + 1) * B], T.yt[:, b * B:(b + 1) * B]).then_inc(S.st, 16)
+        g.sync.wait_ge(S.st, 64)
+        g.wait_ge(S.loc, loc[0])
+        return
+
+    if core in mids:
+        idx = mids.index(core)
+        _, c0, w = middle[idx]
+        kb = w // 16
+        K = NR * kb
+        g.iota(T.pi[:, 0:1], [[0, 1]], 0, 1).then_inc(S.gi, 1)
+        g.iota(T.rr[:, 0:K], [[1, NR], [0, kb]], 0, 0, allow_small_or_imprecise_dtypes=True).then_inc(S.gi, 1)
+        g.iota(T.kk[:, 0:K], [[0, NR], [16, kb]], 0, 0, allow_small_or_imprecise_dtypes=True).then_inc(S.gi, 1)
+    for u in units:
+        if relay(u) == core:
+            w4 = 4 * units[u][1]
+            g.wait_ge(S["u%d" % u[2]], unit_engines(u, ch, rc, relay, topo))
+            send_unit(u, T.rel, u[2] * w4)
+    if core in mids:
+        V = g.vector
+        p15(3)
+        vdo(V.tensor_scalar(T.cc[:, 0:K], T.kk[:, 0:K], T.pf[:, :], None, A.add))
+        vdo(V.tensor_scalar(T.col[:, 0:K], T.kk[:, 0:K], T.pf[:, :], float(c0), A.add, A.add))
+        vwait()
+        V.wait_ge(S.hs, count(sum(engines(topo, rc, [p for p, _ in pairs[ch]]))))
+        vdo(V.tensor_scalar(T.fi[:, :], T.hb[:, 0:1], W - 1, None, A.bitwise_and))
+        vdo(V.tensor_scalar(T.qi[:, :], T.hb[:, 0:1], W.bit_length() - 1, None, A.arith_shift_right))
+        vwait()
+        vdo(V.tensor_copy(T.ff[:, :], T.fi[:, :]))
+        vdo(V.tensor_copy(T.qf[:, :], T.qi[:, :]))
+        vwait()
+        vdo(V.tensor_scalar(T.t0[:, 0:K], T.col[:, 0:K], T.ff[:, :], T.qf[:, :], A.is_lt, A.add))
+        vwait()
+        vdo(V.tensor_tensor(T.t1[:, 0:K], T.t0[:, 0:K], T.rr[:, 0:K], A.add))
+        vwait()
+        vdo(V.tensor_scalar(T.t2[:, 0:K], T.t1[:, 0:K], float(NR), -float(NR), A.is_ge, A.mult))
+        vwait()
+        vdo(V.tensor_tensor(T.t3[:, 0:K], T.t1[:, 0:K], T.t2[:, 0:K], A.add))
+        vwait()
+        vdo(V.tensor_scalar(T.t0[:, 0:K], T.t3[:, 0:K], float(w), None, A.mult))
+        vwait()
+        vdo(V.tensor_tensor(T.t1[:, 0:K], T.t0[:, 0:K], T.cc[:, 0:K], A.add))
+        vwait()
+        vdo(V.tensor_copy(T.off[:, 0:K], T.t1[:, 0:K]))
+        vwait()
+        groups = phase2(idx)
+        arrivals = 2 * NR
+        V.wait_ge(S.arr, arrivals)
+        g.scalar.wait_ge(S.vc, vstep[0])
+        g.scalar.wait_ge(S.arr, arrivals)
+
+        def part(gr):
+            return (T.sel[:, gr * 4 * w:(gr + 1) * 4 * w],
+                    T.win[:, 0:NR * w].indirect(T.off[:, gr * 4 * kb:(gr + 1) * 4 * kb]))
+        o, i_ = part(groups[0])
+        V.tensor_copy(o, i_).then_inc(S.sa, 1)
+        o, i_ = part(groups[1])
+        g.scalar.activation(o, i_, F.Copy).then_inc(S.sb, 1)
+        o, i_ = part(groups[2])
+        V.tensor_copy(o, i_).then_inc(S.sc, 1)
+
+        def send(ranks):
+            masks = deal(engines(topo, core, rank_cores), len(ranks))
+            tr = [copy_to(topo, rank_cores[r], T.sel[:, r * w:(r + 1) * w], T.z[:, c0:c0 + w], mk, S.zs)
+                  for r, mk in zip(ranks, masks)]
+            g.remote_dma_fused(tr, local_sem=S.loc)
+            loc[0] += sum(count(mk) for mk in masks)
+        g.wait_ge(S.sa, 1)
+        g.wait_ge(S.sb, 1)
+        send([4 * gr + i for gr in groups[0:2] for i in range(4)])
+        g.wait_ge(S.sc, 1)
+        send([4 * groups[2] + i for i in range(4)])
+    if loc[0]:
+        g.wait_ge(S.loc, loc[0])
+
+
+def unit_engines(u, ch, rc, relay, topo):
+    for chunk in CHUNKS:
+        if u in chunk:
+            out = [v for v in chunk if relay(v) != rc]
+            out.sort(key=lambda v: topo.die(relay(v)) != topo.die(rc))
+            bits = engines(topo, rc, [relay(v) for v in out])
+            masks = deal(bits[1::2] + bits[0::2], len(out))
+            return count(masks[out.index(u)])

@@ -4,20 +4,18 @@ from concourse.mybir import AluOpType as A, ActivationFunctionType as F
 CORES = 128
 W = 2048
 NR = 12
-WIDTH = {"big": (48, 48, 48, 32), "small": (48, 48, 32, 32)}
-CHUNKS = [
-    [(0, "big", 0), (1, "big", 0), (2, "big", 0), (0, "small", 0), (1, "small", 0)],
-    [(3, "big", 0), (3, "big", 1), (2, "small", 0), (3, "small", 0)],
-    [(0, "big", 1), (1, "big", 1), (2, "big", 1)],
-]
+C = 32
+KB = C // 16
+K = NR * KB
+B = 512
 
 SCRATCH = {
     "xt": ("sbuf", [128, 2048], "float32"),
-    "rel": ("sbuf", [128, 384], "float32"),
-    "win": ("sbuf", [128, 576], "float32"),
-    "sel": ("sbuf", [128, 576], "float32"),
+    "xr": ("sbuf", [128, 2048], "float32"),
+    "rel": ("sbuf", [128, 256], "float32"),
+    "win": ("sbuf", [128, 384], "float32"),
+    "sel": ("sbuf", [128, 384], "float32"),
     "z": ("sbuf", [128, 2048], "float32"),
-    "yt": ("sbuf", [128, 2048], "float32"),
     "h1": ("sbuf", [128, 2], "int32"),
     "hb": ("sbuf", [128, 2], "int32"),
     "pi": ("sbuf", [128, 2], "int32"),
@@ -26,27 +24,28 @@ SCRATCH = {
     "qi": ("sbuf", [128, 1], "int32"),
     "ff": ("sbuf", [128, 1], "float32"),
     "qf": ("sbuf", [128, 1], "float32"),
-    "rr": ("sbuf", [128, 36], "float32"),
-    "kk": ("sbuf", [128, 36], "float32"),
-    "cc": ("sbuf", [128, 36], "float32"),
-    "col": ("sbuf", [128, 36], "float32"),
-    "t0": ("sbuf", [128, 36], "float32"),
-    "t1": ("sbuf", [128, 36], "float32"),
-    "t2": ("sbuf", [128, 36], "float32"),
-    "t3": ("sbuf", [128, 36], "float32"),
-    "off": ("sbuf", [128, 36], "uint16"),
+    "rr": ("sbuf", [128, K], "float32"),
+    "kk": ("sbuf", [128, K], "float32"),
+    "cc": ("sbuf", [128, K], "float32"),
+    "col": ("sbuf", [128, K], "float32"),
+    "t0": ("sbuf", [128, K], "float32"),
+    "t1": ("sbuf", [128, K], "float32"),
+    "t2": ("sbuf", [128, K], "float32"),
+    "t3": ("sbuf", [128, K], "float32"),
+    "off": ("sbuf", [128, K], "uint16"),
     "rk": ("sbuf", [128, 128], "int32"),
     "rj": ("sbuf", [128, 128], "int32"),
     "rm": ("sbuf", [128, 128], "int32"),
     "roff": ("sbuf", [128, 128], "uint16"),
 }
-SEMAPHORES = ["hld", "hbs", "hs", "gi", "vc", "u0", "u1", "arr", "sa", "sb", "sc", "loc", "x0", "x1", "x2", "zs",
+SEMAPHORES = ["hld", "hbs", "hs", "gi", "vc", "u0", "u1", "arr", "s0", "s1", "s2", "loc", "xs", "z0", "z1", "z2",
               "r0", "r1", "r2", "r3", "st"]
 
 
 def make_plan(T, topo):
     rank_cores = list(T.cores)
-    chips = [topo.chip(c) for c in rank_cores]
+    rank_of_chip = {topo.chip(c): i for i, c in enumerate(rank_cores)}
+    chips = sorted({topo.chip(c) for c in range(CORES)}, key=lambda a: (a not in rank_of_chip, a))
     planes = []
     for ch in chips:
         for pl in planes:
@@ -55,34 +54,38 @@ def make_plan(T, topo):
                 break
         else:
             planes.append([ch])
-    planes.sort(key=len)
-    plane = {"small": planes[0], "big": planes[1]}
-    plane_of = {ch: n for n in plane for ch in plane[n]}
+    plane_of = {ch: n for n, pl in enumerate(planes) for ch in pl}
     pairs = {}
-    for rc, ch in zip(rank_cores, chips):
+    for ch in chips:
         mine = [c for c in range(CORES) if topo.chip(c) == ch]
-        ports = [c for c in mine if all(topo.may_write(c, d) for d in rank_cores)]
+        rc = rank_cores[rank_of_chip[ch]] if ch in rank_of_chip else mine[0]
+        ports = [c for c in mine if all(c == d or topo.may_write(c, d) for d in range(CORES))]
         rest = [c for c in mine if c not in ports and c != rc] + [rc]
         out = []
-        for dd in sorted({topo.die(c) for c in mine}, key=lambda d: d == topo.die(rc)):
+        for dd in sorted({topo.die(c) for c in mine}):
             out += list(zip([c for c in ports if topo.die(c) == dd], [c for c in rest if topo.die(c) == dd]))
         pairs[ch] = out
-    units, col = {}, 0
-    spans = []
-    for chunk in CHUNKS:
-        start = col
-        for u in chunk:
-            k, pl, half = u
-            w = WIDTH[pl][k]
-            units[u] = (col, w, plane[pl][4 * half:4 * half + 4])
-            col += 4 * w
-        spans.append((start, col))
-    middle = []
+    units = {}
+    for half in range(2):
+        for pl in range(2):
+            for k in range(4):
+                units[half, pl, k] = (len(units) * 4 * C, planes[pl][4 * half:4 * half + 4])
+    middle = {}
     for u in units:
-        c0, w, chs = units[u]
+        c0, chs = units[u]
         for i, ch in enumerate(chs):
-            middle.append((pairs[ch][u[0]][0], c0 + i * w, w))
-    return rank_cores, chips, plane_of, pairs, units, spans, middle
+            middle[pairs[ch][u[2]][0]] = c0 + i * C
+    via = {}
+    for pl in planes:
+        via.update(zip([c for c in pl if c in rank_of_chip], [c for c in pl if c not in rank_of_chip]))
+    return rank_cores, rank_of_chip, plane_of, pairs, units, middle, via
+
+
+THIRDS = [(0, 5 * 4 * C), (5 * 4 * C, 11 * 4 * C), (11 * 4 * C, W)]
+
+
+def third(c0):
+    return [a <= c0 < b for a, b in THIRDS].index(True)
 
 
 def engines(topo, src, dsts):
@@ -112,202 +115,184 @@ def count(m):
     return bin(m).count("1")
 
 
-def copy_to(topo, dst, src_ap, dst_ap, mask, sem):
-    rid, pid, _ = topo.addr(dst)
-    return RemoteDMATransfer(dst_ids=[DstId(rid=rid, pnc=pid)], dma_engine_mask=mask, remote_sem=sem, src=src_ap,
-                             dst=dst_ap)
-
-
-def phase2(idx):
-    a = idx % 3
-    return [a, (a + 1) % 3, (a + 2) % 3]
-
-
 def rank_program(g, core, T, topo):
-    rank_cores, chips, plane_of, pairs, units, spans, middle = make_plan(T, topo)
+    rank_cores, rank_of_chip, plane_of, pairs, units, middle, via = make_plan(T, topo)
     ch = topo.chip(core)
-    if ch not in pairs:
-        return
     rank = T.rank_of(core)
-    src_rank = chips.index(ch)
-    rc = rank_cores[src_rank]
     S = T.sem
-    mids = [m[0] for m in middle]
+    V = g.vector
     loc = [0]
     vstep = [0]
+    src_rank = rank_of_chip.get(ch)
+    rc = None if src_rank is None else rank_cores[src_rank]
+    ports = [p for p, _ in pairs[ch]]
+
+    def send(tr):
+        g.remote_dma_fused(tr, local_sem=S.loc)
+        loc[0] += sum(count(t[0]) for t in masks_of[-1])
+
+    masks_of = []
+
+    def fused(items):
+        tr = []
+        for m, dsts, src, land, sem in items:
+            ids = []
+            for d in dsts:
+                rid, pid, _ = topo.addr(d)
+                ids.append(DstId(rid=rid, pnc=pid))
+            tr.append(RemoteDMATransfer(dst_ids=ids, dma_engine_mask=m, remote_sem=sem, srcs=[src],
+                                        dsts=[land for d in dsts]))
+        g.remote_dma_fused(tr, local_sem=S.loc)
+        loc[0] += sum(count(it[0]) for it in items)
 
     def relay(u):
-        pair = pairs[ch][u[0]]
+        pair = pairs[ch][u[2]]
         return pair[1] if plane_of[ch] == u[1] else pair[0]
+
+    def halves():
+        return (0, 1) if src_rank % 2 == 0 else (1, 0)
+
+    def spread(half):
+        out = [u for u in units if u[0] == half and relay(u) != rc]
+        out.sort(key=lambda u: topo.die(relay(u)) != topo.die(rc))
+        bits = engines(topo, rc, [relay(u) for u in out])
+        return list(zip(out, deal(bits[1::2] + bits[0::2], len(out))))
+
+    def send_unit(u, src, at):
+        dsts = [pairs[y][u[2]][0] for y in units[u][1]]
+        masks = deal(engines(topo, core, dsts), 4)
+        fused([(masks[i], [d], src[:, at + i * C:at + (i + 1) * C], T.win[:, src_rank * C:(src_rank + 1) * C], S.arr)
+               for i, d in enumerate(dsts)])
 
     def vdo(ins):
         ins.then_inc(S.vc, 1)
         vstep[0] += 1
 
     def vwait():
-        g.vector.wait_ge(S.vc, vstep[0])
-
-    def send_unit(u, src, at):
-        c0, w, chs = units[u]
-        dsts = [pairs[y][u[0]][0] for y in chs]
-        masks = deal(engines(topo, core, dsts), 4)
-        tr = [copy_to(topo, d, src[:, at + i * w:at + (i + 1) * w], T.win[:, src_rank * w:(src_rank + 1) * w], masks[i],
-                      S.arr) for i, d in enumerate(dsts)]
-        g.remote_dma_fused(tr, local_sem=S.loc)
-        loc[0] += sum(count(m) for m in masks)
+        V.wait_ge(S.vc, vstep[0])
 
     def p15(n):
-        g.vector.wait_ge(S.gi, n)
-        vdo(g.vector.tensor_scalar(T.pi[:, 1:2], T.pi[:, 0:1], 15, None, A.bitwise_and))
+        V.wait_ge(S.gi, n)
+        vdo(V.tensor_scalar(T.pi[:, 1:2], T.pi[:, 0:1], 15, None, A.bitwise_and))
         vwait()
-        vdo(g.vector.tensor_copy(T.pf[:, :], T.pi[:, 1:2]))
+        vdo(V.tensor_copy(T.pf[:, :], T.pi[:, 1:2]))
         vwait()
 
     if rank is not None:
+        g.sync.dma_start(T.xt[:, :], T.x[:, :]).then_inc(S.xs, 16)
         g.scalar.dma_start(T.h1[0:1, :], T.hh[0:1, :]).then_inc(S.hld, 16)
-        xs = [S.x0, S.x1, S.x2]
-        for n, q in ((0, g.sync), (1, g.scalar), (2, g.sync)):
-            a, b = spans[n]
-            q.dma_start(T.xt[:, a:b], T.x[:, a:b]).then_inc(xs[n], 16)
         g.iota(T.pi[:, 0:1], [[0, 1]], 0, 1).then_inc(S.gi, 1)
         g.iota(T.rk[:, :], [[16, 128]], 0, 0).then_inc(S.gi, 1)
         g.wait_ge(S.hld, 16)
         g.partition_broadcast(T.hb[:, :], T.h1[0:1, :], 128).then_inc(S.hbs, 1)
         g.wait_ge(S.hbs, 1)
-        ports = [p for p, _ in pairs[ch]]
-        m = sum(engines(topo, core, ports))
-        ids = []
-        for p in ports:
-            rid, pid, _ = topo.addr(p)
-            ids.append(DstId(rid=rid, pnc=pid))
-        g.remote_dma_fused([RemoteDMATransfer(dst_ids=ids, dma_engine_mask=m, remote_sem=S.hs, srcs=[T.hb[:, :]],
-                                              dsts=[T.hb[:, :] for p in ports])], local_sem=S.loc)
-        loc[0] += count(m)
-        mine = []
-        for n, chunk in enumerate(CHUNKS):
-            g.wait_ge(xs[n], 16)
-            mine += [u for u in chunk if relay(u) == core]
-            out = [u for u in chunk if relay(u) != core]
-            out.sort(key=lambda u: topo.die(relay(u)) != topo.die(core))
-            bits = engines(topo, core, [relay(u) for u in out])
-            masks = deal(bits[1::2] + bits[0::2], len(out))
-            tr = []
-            for u, mk in zip(out, masks):
-                c0, w, _ = units[u]
-                at = u[2] * 4 * w
-                tr.append(copy_to(topo, relay(u), T.xt[:, c0:c0 + 4 * w], T.rel[:, at:at + 4 * w], mk,
-                                  S["u%d" % u[2]]))
-            g.remote_dma_fused(tr, local_sem=S.loc)
-            loc[0] += sum(count(mk) for mk in masks)
-        for u in mine:
-            send_unit(u, T.xt, units[u][0])
+        dsts = [p for p, _ in pairs[via[ch]]] if ch in via else ports
+        fused([(sum(engines(topo, core, dsts)), dsts, T.hb[:, :], T.hb[:, :], S.hs)])
         p15(2)
-        g.vector.wait_ge(S.hbs, 1)
-        vdo(g.vector.tensor_copy(T.ff[:, :], T.hb[:, 0:1]))
+        V.wait_ge(S.hbs, 1)
+        vdo(V.tensor_copy(T.ff[:, :], T.hb[:, 0:1]))
         vwait()
-        vdo(g.vector.tensor_scalar(T.rj[:, :], T.rk[:, :], T.pf[:, :], T.ff[:, :], A.add, A.add))
+        vdo(V.tensor_scalar(T.rj[:, :], T.rk[:, :], T.pf[:, :], T.ff[:, :], A.add, A.add))
         vwait()
-        vdo(g.vector.tensor_scalar(T.rm[:, :], T.rj[:, :], W - 1, None, A.bitwise_and))
+        vdo(V.tensor_scalar(T.rm[:, :], T.rj[:, :], W - 1, None, A.bitwise_and))
         vwait()
-        vdo(g.vector.tensor_copy(T.roff[:, :], T.rm[:, :]))
+        vdo(V.tensor_copy(T.roff[:, :], T.rm[:, :]))
         vwait()
-        total = 0
-        for idx in range(len(middle)):
-            total += 2 if rank // 4 == phase2(idx)[2] else 1
-        g.vector.wait_ge(S.zs, total)
+        V.wait_ge(S.xs, 16)
         g.scalar.wait_ge(S.vc, vstep[0])
-        g.scalar.wait_ge(S.zs, total)
-        B = W // 4
-        for b in range(4):
-            src = T.z[:, :].indirect(T.roff[:, b * B // 16:(b + 1) * B // 16])
-            dst = T.yt[:, b * B:(b + 1) * B]
-            if b % 2 == 0:
-                g.vector.tensor_copy(dst, src).then_inc(S["r%d" % b], 1)
-            else:
-                g.scalar.activation(dst, src, F.Copy).then_inc(S["r%d" % b], 1)
-        for b in range(4):
-            g.sync.wait_ge(S["r%d" % b], 1)
-            g.sync.dma_start(T.y[:, b * B:(b + 1) * B], T.yt[:, b * B:(b + 1) * B]).then_inc(S.st, 16)
-        g.sync.wait_ge(S.st, 64)
+        g.scalar.wait_ge(S.xs, 16)
+        for half in halves():
+            for b in (2 * half, 2 * half + 1):
+                src = T.xt[:, :].indirect(T.roff[:, b * B // 16:(b + 1) * B // 16])
+                dst = T.xr[:, b * B:(b + 1) * B]
+                if b % 2 == 0:
+                    V.tensor_copy(dst, src).then_inc(S["r%d" % b], 1)
+                else:
+                    g.scalar.activation(dst, src, F.Copy).then_inc(S["r%d" % b], 1)
+        for half in halves():
+            g.wait_ge(S["r%d" % (2 * half)], 1)
+            g.wait_ge(S["r%d" % (2 * half + 1)], 1)
+            fused([(m, [relay(u)], T.xr[:, units[u][0]:units[u][0] + 4 * C], T.rel[:, u[0] * 4 * C:(u[0] + 1) * 4 * C],
+                    S["u%d" % u[0]]) for u, m in spread(half)])
+        for half in halves():
+            for u in units:
+                if u[0] == half and relay(u) == core:
+                    send_unit(u, T.xr, units[u][0])
+        for n in range(3):
+            t = (rank // 4 - n) % 3
+            a, b = THIRDS[t]
+            g.sync.wait_ge(S["z%d" % t], 2 * ((b - a) // C))
+            g.sync.dma_start(T.y[:, a:b], T.z[:, a:b]).then_inc(S.st, 16)
+        g.sync.wait_ge(S.st, 48)
         g.wait_ge(S.loc, loc[0])
         return
 
-    if core in mids:
-        idx = mids.index(core)
-        _, c0, w = middle[idx]
-        kb = w // 16
-        K = NR * kb
+    mid = core in middle
+    if mid:
+        c0 = middle[core]
         g.iota(T.pi[:, 0:1], [[0, 1]], 0, 1).then_inc(S.gi, 1)
-        g.iota(T.rr[:, 0:K], [[1, NR], [0, kb]], 0, 0, allow_small_or_imprecise_dtypes=True).then_inc(S.gi, 1)
-        g.iota(T.kk[:, 0:K], [[0, NR], [16, kb]], 0, 0, allow_small_or_imprecise_dtypes=True).then_inc(S.gi, 1)
-    for u in units:
-        if relay(u) == core:
-            w4 = 4 * units[u][1]
-            g.wait_ge(S["u%d" % u[2]], unit_engines(u, ch, rc, relay, topo))
-            send_unit(u, T.rel, u[2] * w4)
-    if core in mids:
-        V = g.vector
+        g.iota(T.rr[:, :], [[1, NR], [0, KB]], 0, 0, allow_small_or_imprecise_dtypes=True).then_inc(S.gi, 1)
+        g.iota(T.kk[:, :], [[0, NR], [16, KB]], 0, 0, allow_small_or_imprecise_dtypes=True).then_inc(S.gi, 1)
+        k = ports.index(core)
+        if rc is None:
+            home = [a for a in via if via[a] == ch][0]
+            hrc = rank_cores[rank_of_chip[home]]
+            hcount = len(engines(topo, hrc, ports))
+            dst = pairs[home][k][0]
+            g.wait_ge(S.hs, hcount)
+            fused([(sum(engines(topo, core, [dst])), [dst], T.hb[:, :], T.hb[:, :], S.hs)])
+        elif ch in via:
+            hcount = len(engines(topo, pairs[via[ch]][k][0], [core]))
+        else:
+            hcount = len(engines(topo, rc, ports))
+    if rc is not None:
+        for half in halves():
+            for u, m in spread(half):
+                if relay(u) == core:
+                    g.wait_ge(S["u%d" % half], count(m))
+                    send_unit(u, T.rel, half * 4 * C)
+    if mid:
         p15(3)
-        vdo(V.tensor_scalar(T.cc[:, 0:K], T.kk[:, 0:K], T.pf[:, :], None, A.add))
-        vdo(V.tensor_scalar(T.col[:, 0:K], T.kk[:, 0:K], T.pf[:, :], float(c0), A.add, A.add))
+        vdo(V.tensor_scalar(T.cc[:, :], T.kk[:, :], T.pf[:, :], None, A.add))
         vwait()
-        V.wait_ge(S.hs, count(sum(engines(topo, rc, [p for p, _ in pairs[ch]]))))
+        vdo(V.tensor_scalar(T.col[:, :], T.cc[:, :], -1.0, float(W - c0), A.mult, A.add))
+        vwait()
+        V.wait_ge(S.hs, hcount)
         vdo(V.tensor_scalar(T.fi[:, :], T.hb[:, 0:1], W - 1, None, A.bitwise_and))
         vdo(V.tensor_scalar(T.qi[:, :], T.hb[:, 0:1], W.bit_length() - 1, None, A.arith_shift_right))
         vwait()
         vdo(V.tensor_copy(T.ff[:, :], T.fi[:, :]))
         vdo(V.tensor_copy(T.qf[:, :], T.qi[:, :]))
         vwait()
-        vdo(V.tensor_scalar(T.t0[:, 0:K], T.col[:, 0:K], T.ff[:, :], T.qf[:, :], A.is_lt, A.add))
+        vdo(V.tensor_scalar(T.t0[:, :], T.col[:, :], T.ff[:, :], T.qf[:, :], A.is_le, A.add))
         vwait()
-        vdo(V.tensor_tensor(T.t1[:, 0:K], T.t0[:, 0:K], T.rr[:, 0:K], A.add))
+        vdo(V.tensor_tensor(T.t1[:, :], T.t0[:, :], T.rr[:, :], A.add))
         vwait()
-        vdo(V.tensor_scalar(T.t2[:, 0:K], T.t1[:, 0:K], float(NR), -float(NR), A.is_ge, A.mult))
+        vdo(V.tensor_scalar(T.t2[:, :], T.t1[:, :], float(NR), -float(NR), A.is_ge, A.mult))
         vwait()
-        vdo(V.tensor_tensor(T.t3[:, 0:K], T.t1[:, 0:K], T.t2[:, 0:K], A.add))
+        vdo(V.tensor_tensor(T.t3[:, :], T.t1[:, :], T.t2[:, :], A.add))
         vwait()
-        vdo(V.tensor_scalar(T.t0[:, 0:K], T.t3[:, 0:K], float(w), None, A.mult))
+        vdo(V.tensor_scalar(T.t0[:, :], T.t3[:, :], float(C), None, A.mult))
         vwait()
-        vdo(V.tensor_tensor(T.t1[:, 0:K], T.t0[:, 0:K], T.cc[:, 0:K], A.add))
+        vdo(V.tensor_tensor(T.t1[:, :], T.t0[:, :], T.cc[:, :], A.add))
         vwait()
-        vdo(V.tensor_copy(T.off[:, 0:K], T.t1[:, 0:K]))
+        vdo(V.tensor_copy(T.off[:, :], T.t1[:, :]))
         vwait()
-        groups = phase2(idx)
-        arrivals = 2 * NR
-        V.wait_ge(S.arr, arrivals)
+        V.wait_ge(S.arr, 2 * NR)
         g.scalar.wait_ge(S.vc, vstep[0])
-        g.scalar.wait_ge(S.arr, arrivals)
-
-        def part(gr):
-            return (T.sel[:, gr * 4 * w:(gr + 1) * 4 * w],
-                    T.win[:, 0:NR * w].indirect(T.off[:, gr * 4 * kb:(gr + 1) * 4 * kb]))
-        o, i_ = part(groups[0])
-        V.tensor_copy(o, i_).then_inc(S.sa, 1)
-        o, i_ = part(groups[1])
-        g.scalar.activation(o, i_, F.Copy).then_inc(S.sb, 1)
-        o, i_ = part(groups[2])
-        V.tensor_copy(o, i_).then_inc(S.sc, 1)
-
-        def send(ranks):
-            masks = deal(engines(topo, core, rank_cores), len(ranks))
-            tr = [copy_to(topo, rank_cores[r], T.sel[:, r * w:(r + 1) * w], T.z[:, c0:c0 + w], mk, S.zs)
-                  for r, mk in zip(ranks, masks)]
-            g.remote_dma_fused(tr, local_sem=S.loc)
-            loc[0] += sum(count(mk) for mk in masks)
-        g.wait_ge(S.sa, 1)
-        g.wait_ge(S.sb, 1)
-        send([4 * gr + i for gr in groups[0:2] for i in range(4)])
-        g.wait_ge(S.sc, 1)
-        send([4 * groups[2] + i for i in range(4)])
+        g.scalar.wait_ge(S.arr, 2 * NR)
+        order = [(third(c0) + n) % 3 for n in range(3)]
+        for n, gr in enumerate(order):
+            o = T.sel[:, gr * 4 * C:(gr + 1) * 4 * C]
+            src = T.win[:, :].indirect(T.off[:, gr * 4 * KB:(gr + 1) * 4 * KB])
+            if n == 1:
+                g.scalar.activation(o, src, F.Copy).then_inc(S["s%d" % n], 1)
+            else:
+                V.tensor_copy(o, src).then_inc(S["s%d" % n], 1)
+        masks = deal(engines(topo, core, rank_cores), 4)
+        for n, gr in enumerate(order):
+            g.wait_ge(S["s%d" % n], 1)
+            fused([(masks[i], [rank_cores[r]], T.sel[:, r * C:(r + 1) * C], T.z[:, c0:c0 + C], S["z%d" % third(c0)])
+                   for i, r in enumerate(range(4 * gr, 4 * gr + 4))])
     if loc[0]:
         g.wait_ge(S.loc, loc[0])
-
-
-def unit_engines(u, ch, rc, relay, topo):
-    for chunk in CHUNKS:
-        if u in chunk:
-            out = [v for v in chunk if relay(v) != rc]
-            out.sort(key=lambda v: topo.die(relay(v)) != topo.die(rc))
-            bits = engines(topo, rc, [relay(v) for v in out])
-            masks = deal(bits[1::2] + bits[0::2], len(out))
-            return count(masks[out.index(u)])

@@ -5,9 +5,12 @@ CORES = 128
 W = 2048
 NR = 12
 C = 32
+U = 4 * C
+Q = 4 * U
 KB = C // 16
 K = NR * KB
-B = 512
+B = Q // 2
+THIRDS = [(0, 5 * U), (5 * U, 11 * U), (11 * U, W)]
 
 SCRATCH = {
     "xt": ("sbuf", [128, 2048], "float32"),
@@ -38,8 +41,8 @@ SCRATCH = {
     "rm": ("sbuf", [128, 128], "int32"),
     "roff": ("sbuf", [128, 128], "uint16"),
 }
-SEMAPHORES = ["hld", "hbs", "hs", "gi", "vc", "u0", "u1", "arr", "s0", "s1", "s2", "loc", "xs", "z0", "z1", "z2",
-              "r0", "r1", "r2", "r3", "st"]
+SEMAPHORES = ["hld", "hbs", "hs", "gi", "vc", "u0", "u1", "arr", "s0", "s1", "s2", "loc", "xs", "z0", "z1", "z2", "st"]
+SEMAPHORES += ["r%d" % b for b in range(8)]
 
 
 def make_plan(T, topo):
@@ -69,7 +72,7 @@ def make_plan(T, topo):
     for half in range(2):
         for pl in range(2):
             for k in range(4):
-                units[half, pl, k] = (len(units) * 4 * C, planes[pl][4 * half:4 * half + 4])
+                units[half, pl, k] = (len(units) * U, planes[pl][4 * half:4 * half + 4])
     middle = {}
     for u in units:
         c0, chs = units[u]
@@ -79,9 +82,6 @@ def make_plan(T, topo):
     for pl in planes:
         via.update(zip([c for c in pl if c in rank_of_chip], [c for c in pl if c not in rank_of_chip]))
     return rank_cores, rank_of_chip, plane_of, pairs, units, middle, via
-
-
-THIRDS = [(0, 5 * 4 * C), (5 * 4 * C, 11 * 4 * C), (11 * 4 * C, W)]
 
 
 def third(c0):
@@ -127,12 +127,6 @@ def rank_program(g, core, T, topo):
     rc = None if src_rank is None else rank_cores[src_rank]
     ports = [p for p, _ in pairs[ch]]
 
-    def send(tr):
-        g.remote_dma_fused(tr, local_sem=S.loc)
-        loc[0] += sum(count(t[0]) for t in masks_of[-1])
-
-    masks_of = []
-
     def fused(items):
         tr = []
         for m, dsts, src, land, sem in items:
@@ -149,11 +143,12 @@ def rank_program(g, core, T, topo):
         pair = pairs[ch][u[2]]
         return pair[1] if plane_of[ch] == u[1] else pair[0]
 
-    def halves():
-        return (0, 1) if src_rank % 2 == 0 else (1, 0)
+    def quarters():
+        own = plane_of[ch]
+        return [(half, pl) for half in ((0, 1) if src_rank % 2 == 0 else (1, 0)) for pl in (own, 1 - own)]
 
-    def spread(half):
-        out = [u for u in units if u[0] == half and relay(u) != rc]
+    def spread(quarter):
+        out = [u for u in units if u[:2] == quarter and relay(u) != rc]
         out.sort(key=lambda u: topo.die(relay(u)) != topo.die(rc))
         bits = engines(topo, rc, [relay(u) for u in out])
         return list(zip(out, deal(bits[1::2] + bits[0::2], len(out))))
@@ -179,8 +174,8 @@ def rank_program(g, core, T, topo):
         vwait()
 
     if rank is not None:
+        g.sync.dma_start(T.h1[0:1, :], T.hh[0:1, :]).then_inc(S.hld, 16)
         g.sync.dma_start(T.xt[:, :], T.x[:, :]).then_inc(S.xs, 16)
-        g.scalar.dma_start(T.h1[0:1, :], T.hh[0:1, :]).then_inc(S.hld, 16)
         g.iota(T.pi[:, 0:1], [[0, 1]], 0, 1).then_inc(S.gi, 1)
         g.iota(T.rk[:, :], [[16, 128]], 0, 0).then_inc(S.gi, 1)
         g.wait_ge(S.hld, 16)
@@ -201,22 +196,21 @@ def rank_program(g, core, T, topo):
         V.wait_ge(S.xs, 16)
         g.scalar.wait_ge(S.vc, vstep[0])
         g.scalar.wait_ge(S.xs, 16)
-        for half in halves():
-            for b in (2 * half, 2 * half + 1):
+        for half, pl in quarters():
+            first = units[half, pl, 0][0]
+            for b in (first // B, first // B + 1):
                 src = T.xt[:, :].indirect(T.roff[:, b * B // 16:(b + 1) * B // 16])
                 dst = T.xr[:, b * B:(b + 1) * B]
                 if b % 2 == 0:
                     V.tensor_copy(dst, src).then_inc(S["r%d" % b], 1)
                 else:
                     g.scalar.activation(dst, src, F.Copy).then_inc(S["r%d" % b], 1)
-        for half in halves():
-            g.wait_ge(S["r%d" % (2 * half)], 1)
-            g.wait_ge(S["r%d" % (2 * half + 1)], 1)
-            fused([(m, [relay(u)], T.xr[:, units[u][0]:units[u][0] + 4 * C], T.rel[:, u[0] * 4 * C:(u[0] + 1) * 4 * C],
-                    S["u%d" % u[0]]) for u, m in spread(half)])
-        for half in halves():
+                g.wait_ge(S["r%d" % b], 1)
+            fused([(m, [relay(u)], T.xr[:, units[u][0]:units[u][0] + U], T.rel[:, u[0] * U:(u[0] + 1) * U],
+                    S["u%d" % u[0]]) for u, m in spread((half, pl))])
+        for quarter in quarters():
             for u in units:
-                if u[0] == half and relay(u) == core:
+                if u[:2] == quarter and relay(u) == core:
                     send_unit(u, T.xr, units[u][0])
         for n in range(3):
             t = (rank // 4 - n) % 3
@@ -236,8 +230,7 @@ def rank_program(g, core, T, topo):
         k = ports.index(core)
         if rc is None:
             home = [a for a in via if via[a] == ch][0]
-            hrc = rank_cores[rank_of_chip[home]]
-            hcount = len(engines(topo, hrc, ports))
+            hcount = len(engines(topo, rank_cores[rank_of_chip[home]], ports))
             dst = pairs[home][k][0]
             g.wait_ge(S.hs, hcount)
             fused([(sum(engines(topo, core, [dst])), [dst], T.hb[:, :], T.hb[:, :], S.hs)])
@@ -246,11 +239,11 @@ def rank_program(g, core, T, topo):
         else:
             hcount = len(engines(topo, rc, ports))
     if rc is not None:
-        for half in halves():
-            for u, m in spread(half):
+        for quarter in quarters():
+            for u, m in spread(quarter):
                 if relay(u) == core:
-                    g.wait_ge(S["u%d" % half], count(m))
-                    send_unit(u, T.rel, half * 4 * C)
+                    g.wait_ge(S["u%d" % u[0]], count(m))
+                    send_unit(u, T.rel, u[0] * U)
     if mid:
         p15(3)
         vdo(V.tensor_scalar(T.cc[:, :], T.kk[:, :], T.pf[:, :], None, A.add))

@@ -6,11 +6,9 @@ W = 2048
 NR = 12
 C = 32
 U = 4 * C
-Q = 4 * U
 KB = C // 16
 K = NR * KB
-B = Q // 2
-THIRDS = [(0, 5 * U), (5 * U, 11 * U), (11 * U, W)]
+PARTS = [(0, 3 * U), (3 * U, 5 * U), (5 * U, 8 * U), (8 * U, 11 * U), (11 * U, 13 * U), (13 * U, 16 * U)]
 
 SCRATCH = {
     "xt": ("sbuf", [128, 2048], "float32"),
@@ -41,8 +39,8 @@ SCRATCH = {
     "rm": ("sbuf", [128, 128], "int32"),
     "roff": ("sbuf", [128, 128], "uint16"),
 }
-SEMAPHORES = ["hld", "hbs", "hs", "gi", "vc", "u0", "u1", "arr", "s0", "s1", "s2", "loc", "xs", "z0", "z1", "z2", "st"]
-SEMAPHORES += ["r%d" % b for b in range(8)]
+SEMAPHORES = ["hld", "hbs", "hs", "gi", "vc", "u0", "u1", "arr", "s0", "s1", "s2", "loc", "xs", "st0", "st1"]
+SEMAPHORES += ["z%d" % t for t in range(6)] + ["r%d" % b for b in range(5)]
 
 
 def make_plan(T, topo):
@@ -68,24 +66,22 @@ def make_plan(T, topo):
         for dd in sorted({topo.die(c) for c in mine}):
             out += list(zip([c for c in ports if topo.die(c) == dd], [c for c in rest if topo.die(c) == dd]))
         pairs[ch] = out
-    units = {}
+    units, middle = {}, {}
     for half in range(2):
         for pl in range(2):
             for k in range(4):
-                units[half, pl, k] = (len(units) * U, planes[pl][4 * half:4 * half + 4])
-    middle = {}
-    for u in units:
-        c0, chs = units[u]
-        for i, ch in enumerate(chs):
-            middle[pairs[ch][u[2]][0]] = c0 + i * C
+                c0 = len(units) * U
+                mids = [pairs[ch][k - k % 2 + half][0] for ch in planes[pl][4 * (k % 2):4 * (k % 2) + 4]]
+                units[half, pl, k] = (c0, mids)
+                middle.update({c: c0 + i * C for i, c in enumerate(mids)})
     via = {}
     for pl in planes:
         via.update(zip([c for c in pl if c in rank_of_chip], [c for c in pl if c not in rank_of_chip]))
     return rank_cores, rank_of_chip, plane_of, pairs, units, middle, via
 
 
-def third(c0):
-    return [a <= c0 < b for a, b in THIRDS].index(True)
+def part_of(c0):
+    return [a <= c0 < b for a, b in PARTS].index(True)
 
 
 def engines(topo, src, dsts):
@@ -143,18 +139,22 @@ def rank_program(g, core, T, topo):
         pair = pairs[ch][u[2]]
         return pair[1] if plane_of[ch] == u[1] else pair[0]
 
-    def quarters():
+    def groups():
         own = plane_of[ch]
-        return [(half, pl) for half in ((0, 1) if src_rank % 2 == 0 else (1, 0)) for pl in (own, 1 - own)]
+        out = []
+        for half, pl in [(half, pl) for half in range(2) for pl in (own, 1 - own)]:
+            us = [(half, pl, k) for k in range(4)]
+            out += [us] if out else [us[:2], us[2:]]
+        return out
 
-    def spread(quarter):
-        out = [u for u in units if u[:2] == quarter and relay(u) != rc]
+    def spread(group):
+        out = [u for u in group if relay(u) != rc]
         out.sort(key=lambda u: topo.die(relay(u)) != topo.die(rc))
         bits = engines(topo, rc, [relay(u) for u in out])
         return list(zip(out, deal(bits[1::2] + bits[0::2], len(out))))
 
     def send_unit(u, src, at):
-        dsts = [pairs[y][u[2]][0] for y in units[u][1]]
+        dsts = units[u][1]
         masks = deal(engines(topo, core, dsts), 4)
         fused([(masks[i], [d], src[:, at + i * C:at + (i + 1) * C], T.win[:, src_rank * C:(src_rank + 1) * C], S.arr)
                for i, d in enumerate(dsts)])
@@ -196,28 +196,29 @@ def rank_program(g, core, T, topo):
         V.wait_ge(S.xs, 16)
         g.scalar.wait_ge(S.vc, vstep[0])
         g.scalar.wait_ge(S.xs, 16)
-        for half, pl in quarters():
-            first = units[half, pl, 0][0]
-            for b in (first // B, first // B + 1):
-                src = T.xt[:, :].indirect(T.roff[:, b * B // 16:(b + 1) * B // 16])
-                dst = T.xr[:, b * B:(b + 1) * B]
-                if b % 2 == 0:
-                    V.tensor_copy(dst, src).then_inc(S["r%d" % b], 1)
+        for n, group in enumerate(groups()):
+            a, w = units[group[0]][0], len(group) * U // 2
+            for i in range(2):
+                src = T.xt[:, :].indirect(T.roff[:, (a + i * w) // 16:(a + (i + 1) * w) // 16])
+                dst = T.xr[:, a + i * w:a + (i + 1) * w]
+                if i == 0:
+                    V.tensor_copy(dst, src).then_inc(S["r%d" % n], 1)
                 else:
-                    g.scalar.activation(dst, src, F.Copy).then_inc(S["r%d" % b], 1)
-                g.wait_ge(S["r%d" % b], 1)
+                    g.scalar.activation(dst, src, F.Copy).then_inc(S["r%d" % n], 1)
+            g.wait_ge(S["r%d" % n], 2)
             fused([(m, [relay(u)], T.xr[:, units[u][0]:units[u][0] + U], T.rel[:, u[0] * U:(u[0] + 1) * U],
-                    S["u%d" % u[0]]) for u, m in spread((half, pl))])
-        for quarter in quarters():
-            for u in units:
-                if u[:2] == quarter and relay(u) == core:
-                    send_unit(u, T.xr, units[u][0])
-        for n in range(3):
-            t = (rank // 4 - n) % 3
-            a, b = THIRDS[t]
-            g.sync.wait_ge(S["z%d" % t], 2 * ((b - a) // C))
-            g.sync.dma_start(T.y[:, a:b], T.z[:, a:b]).then_inc(S.st, 16)
-        g.sync.wait_ge(S.st, 48)
+                    S["u%d" % u[0]]) for u, m in spread(group)])
+        for u in units:
+            if relay(u) == core:
+                send_unit(u, T.xr, units[u][0])
+        for half, q in ((0, g.sync), (1, g.scalar)):
+            st = S["st%d" % half]
+            for n in range(3):
+                t = 3 * half + (rank // 4 - n) % 3
+                a, b = PARTS[t]
+                q.wait_ge(S["z%d" % t], 2 * ((b - a) // C))
+                q.dma_start(T.y[:, a:b], T.z[:, a:b]).then_inc(st, 16)
+            q.wait_ge(st, 48)
         g.wait_ge(S.loc, loc[0])
         return
 
@@ -239,8 +240,8 @@ def rank_program(g, core, T, topo):
         else:
             hcount = len(engines(topo, rc, ports))
     if rc is not None:
-        for quarter in quarters():
-            for u, m in spread(quarter):
+        for group in groups():
+            for u, m in spread(group):
                 if relay(u) == core:
                     g.wait_ge(S["u%d" % u[0]], count(m))
                     send_unit(u, T.rel, u[0] * U)
@@ -274,18 +275,21 @@ def rank_program(g, core, T, topo):
         V.wait_ge(S.arr, 2 * NR)
         g.scalar.wait_ge(S.vc, vstep[0])
         g.scalar.wait_ge(S.arr, 2 * NR)
-        order = [(third(c0) + n) % 3 for n in range(3)]
+        t = part_of(c0)
+        order = [(t + n) % 3 for n in range(3)]
         for n, gr in enumerate(order):
-            o = T.sel[:, gr * 4 * C:(gr + 1) * 4 * C]
-            src = T.win[:, :].indirect(T.off[:, gr * 4 * KB:(gr + 1) * 4 * KB])
-            if n == 1:
-                g.scalar.activation(o, src, F.Copy).then_inc(S["s%d" % n], 1)
-            else:
-                V.tensor_copy(o, src).then_inc(S["s%d" % n], 1)
+            for two in range(2):
+                p = 2 * gr + two
+                o = T.sel[:, p * 2 * C:(p + 1) * 2 * C]
+                src = T.win[:, :].indirect(T.off[:, p * 2 * KB:(p + 1) * 2 * KB])
+                if two:
+                    g.scalar.activation(o, src, F.Copy).then_inc(S["s%d" % n], 1)
+                else:
+                    V.tensor_copy(o, src).then_inc(S["s%d" % n], 1)
         masks = deal(engines(topo, core, rank_cores), 4)
         for n, gr in enumerate(order):
-            g.wait_ge(S["s%d" % n], 1)
-            fused([(masks[i], [rank_cores[r]], T.sel[:, r * C:(r + 1) * C], T.z[:, c0:c0 + C], S["z%d" % third(c0)])
+            g.wait_ge(S["s%d" % n], 2)
+            fused([(masks[i], [rank_cores[r]], T.sel[:, r * C:(r + 1) * C], T.z[:, c0:c0 + C], S["z%d" % t])
                    for i, r in enumerate(range(4 * gr, 4 * gr + 4))])
     if loc[0]:
         g.wait_ge(S.loc, loc[0])

from concourse.bass import DstId, RemoteDMATransfer
from concourse.mybir import AluOpType as A, ActivationFunctionType as F

CORES = 128
W = 2048
NR = 12
C = 32
U = 4 * C
KB = C // 16
K = NR * KB
PARTS = [(0, 3 * U), (3 * U, 5 * U), (5 * U, 8 * U), (8 * U, 11 * U), (11 * U, 13 * U), (13 * U, 16 * U)]

SCRATCH = {
    "xt": ("sbuf", [128, 2048], "float32"),
    "xr": ("sbuf", [128, 2048], "float32"),
    "rel": ("sbuf", [128, 256], "float32"),
    "win": ("sbuf", [128, 384], "float32"),
    "sel": ("sbuf", [128, 384], "float32"),
    "z": ("sbuf", [128, 2048], "float32"),
    "h1": ("sbuf", [128, 2], "int32"),
    "hb": ("sbuf", [128, 2], "int32"),
    "pi": ("sbuf", [128, 2], "int32"),
    "pf": ("sbuf", [128, 1], "float32"),
    "fi": ("sbuf", [128, 1], "int32"),
    "qi": ("sbuf", [128, 1], "int32"),
    "ff": ("sbuf", [128, 1], "float32"),
    "qf": ("sbuf", [128, 1], "float32"),
    "rr": ("sbuf", [128, K], "float32"),
    "kk": ("sbuf", [128, K], "float32"),
    "cc": ("sbuf", [128, K], "float32"),
    "col": ("sbuf", [128, K], "float32"),
    "t0": ("sbuf", [128, K], "float32"),
    "t1": ("sbuf", [128, K], "float32"),
    "t2": ("sbuf", [128, K], "float32"),
    "t3": ("sbuf", [128, K], "float32"),
    "off": ("sbuf", [128, K], "uint16"),
    "rk": ("sbuf", [128, 128], "int32"),
    "rj": ("sbuf", [128, 128], "int32"),
    "rm": ("sbuf", [128, 128], "int32"),
    "roff": ("sbuf", [128, 128], "uint16"),
}
SEMAPHORES = ["hld", "hbs", "hs", "gi", "vc", "u0", "u1", "arr", "s0", "s1", "s2", "loc", "xs", "st0", "st1"]
SEMAPHORES += ["z%d" % t for t in range(6)] + ["r%d" % b for b in range(5)]


def make_plan(T, topo):
    rank_cores = list(T.cores)
    rank_of_chip = {topo.chip(c): i for i, c in enumerate(rank_cores)}
    chips = sorted({topo.chip(c) for c in range(CORES)}, key=lambda a: (a not in rank_of_chip, a))
    planes = []
    for ch in chips:
        for pl in planes:
            if topo.same_plane(ch, pl[0]):
                pl.append(ch)
                break
        else:
            planes.append([ch])
    plane_of = {ch: n for n, pl in enumerate(planes) for ch in pl}
    pairs = {}
    for ch in chips:
        mine = [c for c in range(CORES) if topo.chip(c) == ch]
        rc = rank_cores[rank_of_chip[ch]] if ch in rank_of_chip else mine[0]
        ports = [c for c in mine if all(c == d or topo.may_write(c, d) for d in range(CORES))]
        rest = [c for c in mine if c not in ports and c != rc] + [rc]
        out = []
        for dd in sorted({topo.die(c) for c in mine}):
            out += list(zip([c for c in ports if topo.die(c) == dd], [c for c in rest if topo.die(c) == dd]))
        pairs[ch] = out
    units, middle = {}, {}
    for half in range(2):
        for pl in range(2):
            for k in range(4):
                c0 = len(units) * U
                mids = [pairs[ch][k - k % 2 + half][0] for ch in planes[pl][4 * (k % 2):4 * (k % 2) + 4]]
                units[half, pl, k] = (c0, mids)
                middle.update({c: c0 + i * C for i, c in enumerate(mids)})
    via = {}
    for pl in planes:
        via.update(zip([c for c in pl if c in rank_of_chip], [c for c in pl if c not in rank_of_chip]))
    return rank_cores, rank_of_chip, plane_of, pairs, units, middle, via


def part_of(c0):
    return [a <= c0 < b for a, b in PARTS].index(True)


def engines(topo, src, dsts):
    m = -1
    for d in dsts:
        m &= topo.mask(src, d)
    return [1 << e for e in range(m.bit_length()) if m >> e & 1]


def deal(bits, n):
    size = 1
    while 2 * size * n <= len(bits):
        size *= 2
    sizes, left = [size] * n, len(bits) - size * n
    for i in range(n):
        if left >= sizes[i]:
            left -= sizes[i]
            sizes[i] *= 2
    masks, at = [], 0
    for s in sizes:
        masks.append(sum(bits[at:at + s]))
        at += s
    return masks


def count(m):
    return bin(m).count("1")


def rank_program(g, core, T, topo):
    rank_cores, rank_of_chip, plane_of, pairs, units, middle, via = make_plan(T, topo)
    ch = topo.chip(core)
    rank = T.rank_of(core)
    S = T.sem
    V = g.vector
    loc = [0]
    vstep = [0]
    src_rank = rank_of_chip.get(ch)
    rc = None if src_rank is None else rank_cores[src_rank]
    ports = [p for p, _ in pairs[ch]]

    def fused(items):
        tr = []
        for m, dsts, src, land, sem in items:
            ids = []
            for d in dsts:
                rid, pid, _ = topo.addr(d)
                ids.append(DstId(rid=rid, pnc=pid))
            tr.append(RemoteDMATransfer(dst_ids=ids, dma_engine_mask=m, remote_sem=sem, srcs=[src],
                                        dsts=[land for d in dsts]))
        g.remote_dma_fused(tr, local_sem=S.loc)
        loc[0] += sum(count(it[0]) for it in items)

    def relay(u):
        pair = pairs[ch][u[2]]
        return pair[1] if plane_of[ch] == u[1] else pair[0]

    def groups():
        own = plane_of[ch]
        out = []
        for half, pl in [(half, pl) for half in range(2) for pl in (own, 1 - own)]:
            us = [(half, pl, k) for k in range(4)]
            out += [us] if out else [us[:2], us[2:]]
        return out

    def spread(group):
        out = [u for u in group if relay(u) != rc]
        out.sort(key=lambda u: topo.die(relay(u)) != topo.die(rc))
        bits = engines(topo, rc, [relay(u) for u in out])
        return list(zip(out, deal(bits[1::2] + bits[0::2], len(out))))

    def send_unit(u, src, at):
        dsts = units[u][1]
        masks = deal(engines(topo, core, dsts), 4)
        fused([(masks[i], [d], src[:, at + i * C:at + (i + 1) * C], T.win[:, src_rank * C:(src_rank + 1) * C], S.arr)
               for i, d in enumerate(dsts)])

    def vdo(ins):
        ins.then_inc(S.vc, 1)
        vstep[0] += 1

    def vwait():
        V.wait_ge(S.vc, vstep[0])

    def p15(n):
        V.wait_ge(S.gi, n)
        vdo(V.tensor_scalar(T.pi[:, 1:2], T.pi[:, 0:1], 15, None, A.bitwise_and))
        vwait()
        vdo(V.tensor_copy(T.pf[:, :], T.pi[:, 1:2]))
        vwait()

    if rank is not None:
        g.sync.dma_start(T.h1[0:1, :], T.hh[0:1, :]).then_inc(S.hld, 16)
        g.sync.dma_start(T.xt[:, :], T.x[:, :]).then_inc(S.xs, 16)
        g.iota(T.pi[:, 0:1], [[0, 1]], 0, 1).then_inc(S.gi, 1)
        g.iota(T.rk[:, :], [[16, 128]], 0, 0).then_inc(S.gi, 1)
        g.wait_ge(S.hld, 16)
        g.partition_broadcast(T.hb[:, :], T.h1[0:1, :], 128).then_inc(S.hbs, 1)
        g.wait_ge(S.hbs, 1)
        dsts = [p for p, _ in pairs[via[ch]]] if ch in via else ports
        fused([(sum(engines(topo, core, dsts)), dsts, T.hb[:, :], T.hb[:, :], S.hs)])
        p15(2)
        V.wait_ge(S.hbs, 1)
        vdo(V.tensor_copy(T.ff[:, :], T.hb[:, 0:1]))
        vwait()
        vdo(V.tensor_scalar(T.rj[:, :], T.rk[:, :], T.pf[:, :], T.ff[:, :], A.add, A.add))
        vwait()
        vdo(V.tensor_scalar(T.rm[:, :], T.rj[:, :], W - 1, None, A.bitwise_and))
        vwait()
        vdo(V.tensor_copy(T.roff[:, :], T.rm[:, :]))
        vwait()
        V.wait_ge(S.xs, 16)
        g.scalar.wait_ge(S.vc, vstep[0])
        g.scalar.wait_ge(S.xs, 16)
        for n, group in enumerate(groups()):
            a, w = units[group[0]][0], len(group) * U // 2
            for i in range(2):
                src = T.xt[:, :].indirect(T.roff[:, (a + i * w) // 16:(a + (i + 1) * w) // 16])
                dst = T.xr[:, a + i * w:a + (i + 1) * w]
                if i == 0:
                    V.tensor_copy(dst, src).then_inc(S["r%d" % n], 1)
                else:
                    g.scalar.activation(dst, src, F.Copy).then_inc(S["r%d" % n], 1)
            g.wait_ge(S["r%d" % n], 2)
            fused([(m, [relay(u)], T.xr[:, units[u][0]:units[u][0] + U], T.rel[:, u[0] * U:(u[0] + 1) * U],
                    S["u%d" % u[0]]) for u, m in spread(group)])
        for u in units:
            if relay(u) == core:
                send_unit(u, T.xr, units[u][0])
        for half, q in ((0, g.sync), (1, g.scalar)):
            st = S["st%d" % half]
            for n in range(3):
                t = 3 * half + (rank // 4 - n) % 3
                a, b = PARTS[t]
                q.wait_ge(S["z%d" % t], 2 * ((b - a) // C))
                q.dma_start(T.y[:, a:b], T.z[:, a:b]).then_inc(st, 16)
            q.wait_ge(st, 48)
        g.wait_ge(S.loc, loc[0])
        return

    mid = core in middle
    if mid:
        c0 = middle[core]
        g.iota(T.pi[:, 0:1], [[0, 1]], 0, 1).then_inc(S.gi, 1)
        g.iota(T.rr[:, :], [[1, NR], [0, KB]], 0, 0, allow_small_or_imprecise_dtypes=True).then_inc(S.gi, 1)
        g.iota(T.kk[:, :], [[0, NR], [16, KB]], 0, 0, allow_small_or_imprecise_dtypes=True).then_inc(S.gi, 1)
        k = ports.index(core)
        if rc is None:
            home = [a for a in via if via[a] == ch][0]
            hcount = len(engines(topo, rank_cores[rank_of_chip[home]], ports))
            dst = pairs[home][k][0]
            g.wait_ge(S.hs, hcount)
            fused([(sum(engines(topo, core, [dst])), [dst], T.hb[:, :], T.hb[:, :], S.hs)])
        elif ch in via:
            hcount = len(engines(topo, pairs[via[ch]][k][0], [core]))
        else:
            hcount = len(engines(topo, rc, ports))
    if rc is not None:
        for group in groups():
            for u, m in spread(group):
                if relay(u) == core:
                    g.wait_ge(S["u%d" % u[0]], count(m))
                    send_unit(u, T.rel, u[0] * U)
    if mid:
        p15(3)
        vdo(V.tensor_scalar(T.cc[:, :], T.kk[:, :], T.pf[:, :], None, A.add))
        vwait()
        vdo(V.tensor_scalar(T.col[:, :], T.cc[:, :], -1.0, float(W - c0), A.mult, A.add))
        vwait()
        V.wait_ge(S.hs, hcount)
        vdo(V.tensor_scalar(T.fi[:, :], T.hb[:, 0:1], W - 1, None, A.bitwise_and))
        vdo(V.tensor_scalar(T.qi[:, :], T.hb[:, 0:1], W.bit_length() - 1, None, A.arith_shift_right))
        vwait()
        vdo(V.tensor_copy(T.ff[:, :], T.fi[:, :]))
        vdo(V.tensor_copy(T.qf[:, :], T.qi[:, :]))
        vwait()
        vdo(V.tensor_scalar(T.t0[:, :], T.col[:, :], T.ff[:, :], T.qf[:, :], A.is_le, A.add))
        vwait()
        vdo(V.tensor_tensor(T.t1[:, :], T.t0[:, :], T.rr[:, :], A.add))
        vwait()
        vdo(V.tensor_scalar(T.t2[:, :], T.t1[:, :], float(NR), -float(NR), A.is_ge, A.mult))
        vwait()
        vdo(V.tensor_tensor(T.t3[:, :], T.t1[:, :], T.t2[:, :], A.add))
        vwait()
        vdo(V.tensor_scalar(T.t0[:, :], T.t3[:, :], float(C), None, A.mult))
        vwait()
        vdo(V.tensor_tensor(T.t1[:, :], T.t0[:, :], T.cc[:, :], A.add))
        vwait()
        vdo(V.tensor_copy(T.off[:, :], T.t1[:, :]))
        vwait()
        V.wait_ge(S.arr, 2 * NR)
        g.scalar.wait_ge(S.vc, vstep[0])
        g.scalar.wait_ge(S.arr, 2 * NR)
        t = part_of(c0)
        order = [(t + n) % 3 for n in range(3)]
        for n, gr in enumerate(order):
            for two in range(2):
                p = 2 * gr + two
                o = T.sel[:, p * 2 * C:(p + 1) * 2 * C]
                src = T.win[:, :].indirect(T.off[:, p * 2 * KB:(p + 1) * 2 * KB])
                if two:
                    g.scalar.activation(o, src, F.Copy).then_inc(S["s%d" % n], 1)
                else:
                    V.tensor_copy(o, src).then_inc(S["s%d" % n], 1)
        masks = deal(engines(topo, core, rank_cores), 4)
        for n, gr in enumerate(order):
            g.wait_ge(S["s%d" % n], 2)
            fused([(masks[i], [rank_cores[r]], T.sel[:, r * C:(r + 1) * C], T.z[:, c0:c0 + C], S["z%d" % t])
                   for i, r in enumerate(range(4 * gr, 4 * gr + 4))])
    if loc[0]:
        g.wait_ge(S.loc, loc[0])
